import numpy as np
import ml_dtypes


def mxq(x, axis, fmt="e4m3"):
    dtype, down = {"e4m3": (ml_dtypes.float8_e4m3fn, 7), "e5m2": (ml_dtypes.float8_e5m2, 14)}[fmt]
    v = np.moveaxis(np.asarray(x, np.float32).astype(ml_dtypes.bfloat16).astype(np.float64), axis, -1)
    blocks = v.reshape(v.shape[:-1] + (-1, 32))
    amax = np.abs(blocks).max(-1, keepdims=True)
    byte = np.maximum(np.where(amax > 0, np.frexp(amax)[1] - 1 + 127, 0) - down, 1)
    scale = np.exp2(byte - 127.0)
    codes = (blocks / scale).astype(np.float32).astype(dtype).astype(np.float64)
    return np.moveaxis((codes * scale).reshape(v.shape), -1, axis)


WIDE = False


def mx_kscale(k):
    if not WIDE:
        return np.ones(k)
    levels = np.array([10, -10, 5, -5, 0])
    if k % 512:
        return np.exp2(np.random.permutation(np.resize(levels, k // 32))).repeat(32)
    a = np.empty((k // 512, 16))
    for p in range(k // 512):
        a[p, :8] = np.random.permutation(np.resize(levels, 8))
        for g in range(8):
            far = levels[np.abs(levels - a[p, g]) >= 10]
            a[p, g + 8] = far[np.random.randint(len(far))]
    return np.exp2(a.ravel()).repeat(32)


BF16 = ml_dtypes.bfloat16


def bf(x):
    return np.asarray(x, np.float32).astype(BF16)


def f64(x):
    return np.asarray(x).astype(np.float64)

def planes(Y):
    n, m = Y.shape
    b = f64(bf(Y)).reshape(n // 32, 32, m)
    amax = np.abs(b).max(1)
    byte = np.clip(np.where(amax > 0, np.frexp(amax)[1] - 1 + 127 - 7, 1), 1, 254)
    codes = (b * np.exp2(127.0 - byte)[:, None, :]).reshape(n, m).astype(np.float32).astype(ml_dtypes.float8_e4m3fn).view(np.uint8)
    words = codes.reshape(n // 512, 128, 4, m).transpose(0, 1, 3, 2)
    return np.ascontiguousarray(words), np.ascontiguousarray(byte.astype(np.uint8).reshape(n // 512, 16, m))


N, S, R = 1024, 1024, 1024


def scale_rows(weights, field):
    return weights[:, None] * field


def setup_inputs():
    s, t = mx_kscale(N), mx_kscale(N)
    return {
        "gs": bf(np.random.standard_normal((N, S))),
        "g0": bf(np.random.standard_normal((N, N)) / np.sqrt(N) / s[None, :]),
        "gr": bf(np.random.standard_normal((R, N)) / np.sqrt(N) / t[None, :]),
        "v": bf(np.random.standard_normal(N) * s),
        "dv": bf(np.random.standard_normal(N) * t),
        "u0": bf(np.random.uniform(0.5, 2.0, (R, S))),
        "dobs": bf(np.random.uniform(0.5, 2.0, (R, S))),
    }


def core(gs, g0, gr, v, dv, u0, dobs):
    gs, u0, dobs = f64(gs), f64(u0), f64(dobs)
    p = scale_rows(f64(v), gs)
    u = gs + (mxq(f64(g0), 1, "e4m3") @ mxq(p, 0, "e4m3"))
    q = scale_rows(f64(dv), u)
    du = mxq(f64(gr), 1, "e4m3") @ mxq(q, 0, "e4m3")
    phi = du / u0
    return phi + np.log(u0) - np.log(dobs)


def reference(gs, g0, gr, v, dv, u0, dobs):
    R_out = core(gs, g0, gr, v, dv, u0, dobs)
    words, scales = planes(R_out)
    return R_out, words, scales

@@ -1,0 +1,282 @@
+from contextlib import ExitStack
+
+import concourse.mybir as mybir
+from concourse.masks import make_identity
+
+N, S, R = 1024, 1024, 1024
+FLOPS = 2 * N * N * S + 2 * R * N * S
+
+F32 = mybir.dt.float32
+BF16 = mybir.dt.bfloat16
+U32 = mybir.dt.uint32
+I32 = mybir.dt.int32
+U8 = mybir.dt.uint8
+FP8X4 = mybir.dt.float8_e4m3fn_x4
+ALU = mybir.AluOpType
+ACT = mybir.ActivationFunctionType
+
+P = 128
+T = 4
+G = 2
+H = 2
+W = 512
+
+
+def tile_laplacedomaindistortedbornrytovresidual_x1_kernel(tc, gs, g0, gr, v, dv, u0, dobs, out, words, scales):
+    nc = tc.nc
+    with ExitStack() as ctx:
+        keep = ctx.enter_context(tc.tile_pool(name="keep", bufs=1))
+        work = ctx.enter_context(tc.tile_pool(name="work", bufs=2))
+        psum = ctx.enter_context(tc.psum_pool(name="psum", bufs=8))
+        ctx.enter_context(tc.manual_schedule())
+
+        v_col = keep.tile([P, G, T], BF16, name="v_col")
+        dv_col = keep.tile([P, G, T], BF16, name="dv_col")
+        nc.scalar.dma_start(out=v_col[:], in_=v.rearrange("(g p t) -> p g t", g=G, t=T))
+        nc.scalar.dma_start(out=dv_col[:], in_=dv.rearrange("(g p t) -> p g t", g=G, t=T))
+
+        gs_sb = keep.tile([P, G, T, S], BF16, name="gs_sb")
+        gs_v = gs.rearrange("(g p t) s -> g p t s", g=G, t=T)
+
+        def load_gs(g, h):
+            cols = slice(W * h, W * h + W)
+            nc.sync.dma_start(out=gs_sb[:, g, :, cols], in_=gs_v[g, :, :, cols])
+
+        def load_rows(src, g, name):
+            tile = keep.tile([P, T, 1024], BF16, name=name)
+            nc.sync.dma_start(out=tile[:], in_=src.rearrange("(g p t) c -> g p t c", g=G, t=T)[g])
+            return tile
+
+        load_gs(0, 0)
+        load_gs(1, 0)
+        g0_sb = [load_rows(g0, 0, "g0_sb0")]
+        load_gs(0, 1)
+        load_gs(1, 1)
+        g0_sb.append(load_rows(g0, 1, "g0_sb1"))
+        u0_sb = [load_rows(u0, 0, "u0_sb0")]
+        do_sb = [load_rows(dobs, 0, "do_sb0")]
+        gr_sb = [load_rows(gr, 0, "gr_sb0"), load_rows(gr, 1, "gr_sb1")]
+        u0_sb.append(load_rows(u0, 1, "u0_sb1"))
+        do_sb.append(load_rows(dobs, 1, "do_sb1"))
+
+        ident = keep.tile([P, P], F32, name="ident")
+        make_identity(nc, ident[:])
+
+        def operand(name):
+            codes = keep.tile([P, G, 1024], U32, name=name + "_c", align_bytes=64)
+            planes = keep.tile([P, G, 1024], U8, name=name + "_s", align_bytes=64)
+            return codes, planes
+
+        p_c, p_s = operand("p")
+        q_c, q_s = operand("q")
+        g0_c, g0_s = operand("g0")
+        gr_c, gr_s = operand("gr")
+
+        def quant_tile():
+            return work.tile([P, W, T], BF16, name="qin", tag="qin", bufs=6, align_bytes=64)
+
+        def quantise(src, codes, planes, k, c0):
+            nc.vector.quantize_mx(
+                out=codes[:, k, c0 : c0 + W].bitcast(FP8X4),
+                scales=planes[:, k, c0 : c0 + W],
+                in_=src[:].rearrange("p c t -> p (c t)"),
+            )
+
+        def make_p(k, h):
+            dst = quant_tile()
+            nc.vector.tensor_tensor(
+                out=dst[:],
+                in0=gs_sb[:, k, :, W * h : W * h + W].rearrange("p t s -> p s t"),
+                in1=v_col[:, k, :].unsqueeze(1).to_broadcast([P, W, T]),
+                op=ALU.mult,
+            )
+            return dst
+
+        def turn(src, k, half):
+            bank = psum.tile([P, 2, 2, P], F32, name="bank", tag="bank")
+            for i in range(2):
+                w32 = src[:, 2 * half + i, :].bitcast(F32)
+                for u in range(2):
+                    nc.tensor.transpose(bank[:, i, u, :], w32[:, 256 * k + u : 256 * (k + 1) : 2], ident[:])
+            return bank
+
+        def copy_turned(dst, bank, half):
+            d32 = dst[:].rearrange("p c t -> p (c t)").bitcast(F32).rearrange("p (c u) -> p c u", u=2)
+            nc.scalar.copy(
+                out=d32[:, 256 * half : 256 * half + 256, :].rearrange("p (i m) u -> p i m u", i=2),
+                in_=bank[:].rearrange("p i u m -> p i m u"),
+            )
+
+        def turn_group(src):
+            dsts = []
+            for k in range(G):
+                dst = quant_tile()
+                for half in range(2):
+                    copy_turned(dst, turn(src, k, half), half)
+                dsts.append(dst)
+            return dsts
+
+        def product(lc, ls, rc, rs, g, h):
+            banks = []
+            for t in range(T):
+                acc = psum.tile([P, W], F32, name="bank", tag="bank")
+                m0 = W * g + P * t
+                for k in range(G):
+                    nc.tensor.matmul_mx(
+                        out=acc[:],
+                        lhsT=lc[:, k, m0 : m0 + P].bitcast(FP8X4),
+                        lhsT_scale=ls[:, k, m0 : m0 + P],
+                        rhs=rc[:, k, W * h : W * h + W].bitcast(FP8X4),
+                        rhs_scale=rs[:, k, W * h : W * h + W],
+                        start=(k == 0),
+                        stop=(k == G - 1),
+                    )
+                banks.append(acc)
+            return banks
+
+        def make_u(banks, g, h):
+            u = work.tile([P, T, W], F32, name="u", tag="u", bufs=2)
+            for t in range(T):
+                nc.vector.tensor_tensor(
+                    out=u[:, t, :], in0=banks[t][:], in1=gs_sb[:, g, t, W * h : W * h + W], op=ALU.add
+                )
+            return u
+
+        def make_q(u, g):
+            dst = quant_tile()
+            nc.vector.tensor_tensor(
+                out=dst[:],
+                in0=u[:].rearrange("p t s -> p s t"),
+                in1=dv_col[:, g, :].unsqueeze(1).to_broadcast([P, W, T]),
+                op=ALU.mult,
+            )
+            return dst
+
+        lu = {}
+        ld = {}
+
+        def logs(g, h):
+            a = keep.tile([P, T, W], F32, name="lu%d%d" % (g, h))
+            b = keep.tile([P, T, W], F32, name="ld%d%d" % (g, h))
+            cols = slice(W * h, W * h + W)
+            nc.scalar.activation(out=a[:], in_=u0_sb[g][:, :, cols], func=ACT.Ln)
+            nc.scalar.activation(out=b[:], in_=do_sb[g][:, :, cols], func=ACT.Ln)
+            for t in range(T):
+                nc.gpsimd.tensor_tensor(out=b[:, t, :], in0=a[:, t, :], in1=b[:, t, :], op=ALU.subtract)
+            lu[g, h] = a
+            ld[g, h] = b
+
+        def recip(g, h):
+            nc.scalar.activation(out=lu[g, h][:], in_=lu[g, h][:], func=ACT.Exp, scale=-1.0)
+
+        out_v = out.rearrange("(g p t) s -> g p t s", g=G, t=T)
+        o_s = [keep.tile([P, S], U8, name="o_s%d" % g, align_bytes=64) for g in range(G)]
+
+        def phi(banks, g, h):
+            r = lu[g, h]
+            for t in range(T):
+                nc.vector.tensor_tensor(out=r[:, t, :], in0=banks[t][:], in1=r[:, t, :], op=ALU.mult)
+
+        def finish(g, h, c0, cn):
+            r = lu[g, h]
+            cols = slice(c0, c0 + cn)
+            nc.vector.tensor_tensor(out=r[:, :, cols], in0=r[:, :, cols], in1=ld[g, h][:, :, cols], op=ALU.add)
+            nc.sync.dma_start(out=out_v[g, :, :, W * h + c0 : W * h + c0 + cn], in_=r[:, :, cols])
+
+        def round_out(dst, g, h, c0, cn, engine):
+            view = lu[g, h][:, :, c0 : c0 + cn].rearrange("p t s -> p s t")
+            if engine == "scalar":
+                nc.scalar.copy(out=dst[:, c0 : c0 + cn, :], in_=view)
+            else:
+                nc.vector.tensor_copy(out=dst[:, c0 : c0 + cn, :], in_=view)
+
+        def store_planes(src, g, h, c0, cn):
+            codes = work.tile([P, W], U32, name="o_c", tag="o_c", bufs=2, align_bytes=64)
+            s0 = W * h + c0
+            nc.vector.quantize_mx(
+                out=codes[:, c0 : c0 + cn].bitcast(FP8X4),
+                scales=o_s[g][:, s0 : s0 + cn],
+                in_=src[:, c0 : c0 + cn, :].rearrange("p c t -> p (c t)"),
+            )
+            nc.sync.dma_start(
+                out=words[g, :, s0 : s0 + cn, :].rearrange("p m t -> p (m t)").bitcast(I32),
+                in_=codes[:, c0 : c0 + cn].bitcast(I32),
+            )
+
+        def store_scales(g):
+            for q in range(4):
+                nc.sync.dma_start(
+                    out=scales[g, 4 * q : 4 * q + 4, :].bitcast(I32),
+                    in_=o_s[g][32 * q : 32 * q + 4, :].bitcast(I32),
+                )
+
+        pa = [make_p(0, 0), make_p(1, 0)]
+        for k in range(G):
+            quantise(pa[k], p_c, p_s, k, 0)
+        xa = turn_group(g0_sb[0])
+        for k in range(G):
+            quantise(xa[k], g0_c, g0_s, k, 0)
+        t0 = product(g0_c, g0_s, p_c, p_s, 0, 0)
+        pb = [make_p(0, 1), make_p(1, 1)]
+        xb = turn_group(g0_sb[1])
+        for k in range(G):
+            quantise(xb[k], g0_c, g0_s, k, W)
+        t1 = product(g0_c, g0_s, p_c, p_s, 1, 0)
+        u_0 = make_u(t0, 0, 0)
+        for k in range(G):
+            quantise(pb[k], p_c, p_s, k, W)
+        t2 = product(g0_c, g0_s, p_c, p_s, 0, 1)
+        u_1 = make_u(t1, 1, 0)
+        logs(0, 0)
+        logs(0, 1)
+        qa = make_q(u_0, 0)
+        u_2 = make_u(t2, 0, 1)
+        quantise(qa, q_c, q_s, 0, 0)
+        t3 = product(g0_c, g0_s, p_c, p_s, 1, 1)
+        qb = make_q(u_1, 1)
+        u_3 = make_u(t3, 1, 1)
+        quantise(qb, q_c, q_s, 1, 0)
+        ya = turn_group(gr_sb[0])
+        qc = make_q(u_2, 0)
+        for k in range(G):
+            quantise(ya[k], gr_c, gr_s, k, 0)
+        quantise(qc, q_c, q_s, 0, W)
+        yb = turn_group(gr_sb[1])
+        qd = make_q(u_3, 1)
+        for k in range(G):
+            quantise(yb[k], gr_c, gr_s, k, W)
+        quantise(qd, q_c, q_s, 1, W)
+        logs(1, 0)
+        logs(1, 1)
+        order = [(0, 0), (0, 1), (1, 0), (1, 1)]
+        for g, h in order:
+            recip(g, h)
+
+        acc = {}
+        acc[0] = product(gr_c, gr_s, q_c, q_s, 0, 0)
+        phi(acc[0], 0, 0)
+        acc[1] = product(gr_c, gr_s, q_c, q_s, 0, 1)
+        phi(acc[1], 0, 1)
+        rounded = {}
+        for i in range(4):
+            g, h = order[i]
+            rounded[i] = quant_tile()
+            if i < 3:
+                finish(g, h, 0, W)
+                round_out(rounded[i], g, h, 0, W, "scalar")
+            else:
+                finish(g, h, 0, W // 2)
+                round_out(rounded[i], g, h, 0, W // 2, "scalar")
+                finish(g, h, W // 2, W // 2)
+                round_out(rounded[i], g, h, W // 2, W // 2, "vector")
+            if i + 2 < 4:
+                acc[i + 2] = product(gr_c, gr_s, q_c, q_s, order[i + 2][0], order[i + 2][1])
+                phi(acc[i + 2], order[i + 2][0], order[i + 2][1])
+            if i > 0:
+                pg, ph = order[i - 1]
+                store_planes(rounded[i - 1], pg, ph, 0, W)
+                if ph == 1:
+                    store_scales(pg)
+        store_planes(rounded[3], 1, 1, 0, W // 2)
+        store_planes(rounded[3], 1, 1, W // 2, W // 2)
+        store_scales(1)

@@ -20,6 +20,130 @@ T = 4
 G = 2
 H = 2
 W = 512
+ORDER = [
+    ("Lgs", 1, 0),
+    ("ps", 1, 0),
+    ("lead",),
+    ("dv",),
+    ("Lgs", 0, 0, 0, 256),
+    ("Lgs", 0, 0, 256, 256),
+    ("Lgs", 0, 1),
+    ("L", "g0", 0),
+    ("pt", 0, 0, 0, 256),
+    ("ps", 0, 1),
+    ("pi", 0, 1, "S"),
+    ("turn", "g0", 0, 1, "S"),
+    ("L", "u0", 0),
+    ("L", "g0", 1),
+    ("pi", 1, 0, "V"),
+    ("Lgs", 1, 1),
+    ("ln", "u0", 0, 1),
+    ("pt", 0, 0, 256, 256),
+    ("ln", "u0", 0, 0),
+    ("pq", 1, 0),
+    ("pq", 0, 0),
+    ("pq", 0, 1),
+    ("wq", "g0", 0, 1),
+    ("turn", "g0", 0, 0, "V"),
+    ("L", "do", 0),
+    ("wq", "g0", 0, 0),
+    ("turn", "g0", 1, 0, "S"),
+    ("L", "u0", 1),
+    ("ln", "do", 0, 0),
+    ("pt", 1, 1),
+    ("df", 0, 0, 2, "G"),
+    ("mm", "1", 0, 0, 0),
+    ("wq", "g0", 1, 0),
+    ("turn", "g0", 1, 1, "S"),
+    ("L", "do", 1),
+    ("mm", "1", 0, 0, 1),
+    ("pq", 1, 1),
+    ("mm", "1", 0, 1, 0),
+    ("ug", 0, 0, 0),
+    ("ug", 0, 0, 1),
+    ("L", "gr", 1),
+    ("mm", "1", 0, 1, 1),
+    ("ln", "do", 0, 1),
+    ("wq", "g0", 1, 1),
+    ("ln", "do", 1, 1),
+    ("df", 0, 1, 0, "G"),
+    ("mm", "1", 1, 0, 0),
+    ("df", 0, 1, 2, "G"),
+    ("uh", 0, 0),
+    ("ug", 0, 1, 0),
+    ("mm", "1", 1, 0, 1),
+    ("ug", 0, 1, 1),
+    ("ln", "do", 1, 0),
+    ("us", 0, 1, "S"),
+    ("mm", "1", 1, 1, 1),
+    ("ug", 1, 0, 0),
+    ("L", "gr", 0),
+    ("mm", "1", 1, 1, 0),
+    ("ug", 1, 0, 1),
+    ("ug", 1, 1, 0),
+    ("ln", "u0", 1, 1),
+    ("turn", "gr", 1, 1, "V"),
+    ("ln", "u0", 1, 0),
+    ("df", 0, 0, 0, "G"),
+    ("qi", 0, 1, "V"),
+    ("ug", 1, 1, 1),
+    ("qq", 0, 1),
+    ("turn", "gr", 0, 1, "S"),
+    ("us", 1, 0, "S"),
+    ("df", 1, 1, 0, "G"),
+    ("wq", "gr", 0, 1),
+    ("turn", "gr", 1, 0, "S"),
+    ("qi", 1, 0, "S"),
+    ("us", 1, 1, "V"),
+    ("turn", "gr", 0, 0, "S"),
+    ("df", 1, 0, 2, "V"),
+    ("rx", 0, 0),
+    ("df", 1, 0, 0, "V"),
+    ("qq", 0, 0),
+    ("wq", "gr", 1, 0),
+    ("qq", 1, 0),
+    ("wq", "gr", 0, 0),
+    ("rx", 0, 1),
+    ("mm", "2", 0, 0, 1),
+    ("df", 1, 1, 2, "V"),
+    ("qi", 1, 1, "V"),
+    ("rx", 1, 1),
+    ("mm", "2", 0, 0, 0),
+    ("wq", "gr", 1, 1),
+    ("rx", 1, 0),
+    ("qq", 1, 1),
+    ("om", 0, 0, 0),
+    ("mm", "2", 0, 1, 1),
+    ("om", 0, 0, 1),
+    ("mm", "2", 0, 1, 0),
+    ("mm", "2", 1, 0, 0),
+    ("om", 0, 1, 1),
+    ("om", 0, 1, 0),
+    ("pf", 0, 0, 0, 512, "V"),
+    ("mm", "2", 1, 1, 1),
+    ("mm", "2", 1, 0, 1),
+    ("om", 1, 0, 0),
+    ("mm", "2", 1, 1, 0),
+    ("om", 1, 0, 1),
+    ("pf", 0, 1, 0, 512, "G"),
+    ("om", 1, 1, 1),
+    ("om", 1, 1, 0),
+    ("pf", 1, 0, 0, 512, "V"),
+    ("oc", 0, 0, 0, 512, "S"),
+    ("pf", 1, 1, 0, 256, "V"),
+    ("oc", 0, 1, 0, 512, "S"),
+    ("oq", 0, 1, 0, 512),
+    ("pf", 1, 1, 256, 256, "V"),
+    ("oc", 1, 1, 0, 256, "S"),
+    ("oc", 1, 1, 256, 256, "S"),
+    ("oq", 0, 0, 0, 512),
+    ("oc", 1, 0, 0, 512, "V"),
+    ("os", 0),
+    ("oq", 1, 1, 256, 256),
+    ("oq", 1, 0, 0, 512),
+    ("oq", 1, 1, 0, 256),
+    ("os", 1),
+]
 
 
 def tile_laplacedomaindistortedbornrytovresidual_x1_kernel(tc, gs, g0, gr, v, dv, u0, dobs, out, words, scales):
@@ -27,256 +151,254 @@ def tile_laplacedomaindistortedbornrytovresidual_x1_kernel(tc, gs, g0, gr, v, dv
     with ExitStack() as ctx:
         keep = ctx.enter_context(tc.tile_pool(name="keep", bufs=1))
         work = ctx.enter_context(tc.tile_pool(name="work", bufs=2))
-        psum = ctx.enter_context(tc.psum_pool(name="psum", bufs=8))
+        psum = ctx.enter_context(tc.psum_pool(name="psum", bufs=2))
         ctx.enter_context(tc.manual_schedule())
+        tiles = {}
 
         v_col = keep.tile([P, G, T], BF16, name="v_col")
         dv_col = keep.tile([P, G, T], BF16, name="dv_col")
         nc.scalar.dma_start(out=v_col[:], in_=v.rearrange("(g p t) -> p g t", g=G, t=T))
-        nc.scalar.dma_start(out=dv_col[:], in_=dv.rearrange("(g p t) -> p g t", g=G, t=T))
-
-        gs_sb = keep.tile([P, G, T, S], BF16, name="gs_sb")
-        gs_v = gs.rearrange("(g p t) s -> g p t s", g=G, t=T)
-
-        def load_gs(g, h):
-            cols = slice(W * h, W * h + W)
-            nc.sync.dma_start(out=gs_sb[:, g, :, cols], in_=gs_v[g, :, :, cols])
-
-        def load_rows(src, g, name):
-            tile = keep.tile([P, T, 1024], BF16, name=name)
-            nc.sync.dma_start(out=tile[:], in_=src.rearrange("(g p t) c -> g p t c", g=G, t=T)[g])
-            return tile
-
-        load_gs(0, 0)
-        load_gs(1, 0)
-        g0_sb = [load_rows(g0, 0, "g0_sb0")]
-        load_gs(0, 1)
-        load_gs(1, 1)
-        g0_sb.append(load_rows(g0, 1, "g0_sb1"))
-        u0_sb = [load_rows(u0, 0, "u0_sb0")]
-        do_sb = [load_rows(dobs, 0, "do_sb0")]
-        gr_sb = [load_rows(gr, 0, "gr_sb0"), load_rows(gr, 1, "gr_sb1")]
-        u0_sb.append(load_rows(u0, 1, "u0_sb1"))
-        do_sb.append(load_rows(dobs, 1, "do_sb1"))
-
+        dv32 = keep.tile([P, G, T], F32, name="dv32")
         ident = keep.tile([P, P], F32, name="ident")
         make_identity(nc, ident[:])
 
-        def operand(name):
-            codes = keep.tile([P, G, 1024], U32, name=name + "_c", align_bytes=64)
-            planes = keep.tile([P, G, 1024], U8, name=name + "_s", align_bytes=64)
-            return codes, planes
+        gs_sb = keep.tile([P, G, T, S], BF16, name="gs_sb")
+        gs_v = gs.rearrange("(g p t) s -> g p t s", g=G, t=T)
+        out_v = out.rearrange("(g p t) s -> g p t s", g=G, t=T)
 
-        p_c, p_s = operand("p")
-        q_c, q_s = operand("q")
-        g0_c, g0_s = operand("g0")
-        gr_c, gr_s = operand("gr")
+        def cols(h):
+            return slice(W * h, W * h + W)
+
+        def load_gs(g, h, c0=0, cn=W):
+            c = slice(W * h + c0, W * h + c0 + cn)
+            nc.sync.dma_start(out=gs_sb[:, g, :, c], in_=gs_v[g, :, :, c])
+
+        def load_dv():
+            nc.sync.dma_start(out=dv_col[:], in_=dv.rearrange("(g p t) -> p g t", g=G, t=T))
+            nc.gpsimd.tensor_copy(out=dv32[:], in_=dv_col[:])
+
+        def load(which, g):
+            src = {"g0": g0, "gr": gr, "u0": u0, "do": dobs}[which]
+            if which.startswith("g"):
+                tile = work.tile([P, T, 1024], BF16, name="wraw", tag="wraw", bufs=2)
+            else:
+                tile = keep.tile([P, T, 1024], BF16, name=which + str(g))
+            nc.sync.dma_start(out=tile[:], in_=src.rearrange("(g p t) c -> g p t c", g=G, t=T)[g])
+            tiles[which, g] = tile
+
+        codes = {}
+        planes = {}
+        for which in ["p", "q", "g0", "gr"]:
+            for k in range(G):
+                codes[which, k] = keep.tile([P, 1024], U32, name=which + "_c" + str(k), align_bytes=64)
+                planes[which, k] = keep.tile([P, 1024], U8, name=which + "_s" + str(k), align_bytes=64)
+        for g in range(G):
+            planes["o", g] = keep.tile([P, S], U8, name="o_s" + str(g), align_bytes=64)
 
         def quant_tile():
-            return work.tile([P, W, T], BF16, name="qin", tag="qin", bufs=6, align_bytes=64)
+            return work.tile([P, W, T], BF16, name="qin", tag="qin", bufs=8, align_bytes=64)
 
-        def quantise(src, codes, planes, k, c0):
+        def quantise(src, which, k, c0):
             nc.vector.quantize_mx(
-                out=codes[:, k, c0 : c0 + W].bitcast(FP8X4),
-                scales=planes[:, k, c0 : c0 + W],
+                out=codes[which, k][:, c0 : c0 + W].bitcast(FP8X4),
+                scales=planes[which, k][:, c0 : c0 + W],
                 in_=src[:].rearrange("p c t -> p (c t)"),
             )
 
-        def make_p(k, h):
-            dst = quant_tile()
+        def mixed_in(ap):
+            return ap.rearrange("p t (c i) -> p c t i", i=4)
+
+        def mixed_out(ap):
+            return ap.rearrange("p (c i) t -> p c t i", i=4)
+
+        def spread(col, n):
+            return col.unsqueeze(1).unsqueeze(3).to_broadcast([P, n // 4, T, 4])
+
+        def engine_copy(engine, out, in_):
+            if engine == "S":
+                nc.scalar.copy(out=out, in_=in_)
+            elif engine == "V":
+                nc.vector.tensor_copy(out=out, in_=in_)
+            else:
+                nc.gpsimd.tensor_scalar(out=out, in0=in_, scalar1=1.0, scalar2=0.0, op0=ALU.mult, op1=ALU.add)
+
+        def pt(k, h, c0=0, cn=W):
+            if ("p", k, h) not in tiles:
+                tiles["p", k, h] = quant_tile()
+            c = slice(W * h + c0, W * h + c0 + cn)
             nc.vector.tensor_tensor(
-                out=dst[:],
-                in0=gs_sb[:, k, :, W * h : W * h + W].rearrange("p t s -> p s t"),
-                in1=v_col[:, k, :].unsqueeze(1).to_broadcast([P, W, T]),
-                op=ALU.mult,
-            )
-            return dst
-
-        def turn(src, k, half):
-            bank = psum.tile([P, 2, 2, P], F32, name="bank", tag="bank")
-            for i in range(2):
-                w32 = src[:, 2 * half + i, :].bitcast(F32)
-                for u in range(2):
-                    nc.tensor.transpose(bank[:, i, u, :], w32[:, 256 * k + u : 256 * (k + 1) : 2], ident[:])
-            return bank
-
-        def copy_turned(dst, bank, half):
-            d32 = dst[:].rearrange("p c t -> p (c t)").bitcast(F32).rearrange("p (c u) -> p c u", u=2)
-            nc.scalar.copy(
-                out=d32[:, 256 * half : 256 * half + 256, :].rearrange("p (i m) u -> p i m u", i=2),
-                in_=bank[:].rearrange("p i u m -> p i m u"),
+                out=mixed_out(tiles["p", k, h][:, c0 : c0 + cn, :]), in0=mixed_in(gs_sb[:, k, :, c]), in1=spread(v_col[:, k, :], cn), op=ALU.mult
             )
 
-        def turn_group(src):
-            dsts = []
-            for k in range(G):
-                dst = quant_tile()
-                for half in range(2):
-                    copy_turned(dst, turn(src, k, half), half)
-                dsts.append(dst)
-            return dsts
-
-        def product(lc, ls, rc, rs, g, h):
-            banks = []
+        def ps(k, h):
+            pm = work.tile([P, T, W], BF16, name="pm", tag="pm", bufs=2)
             for t in range(T):
-                acc = psum.tile([P, W], F32, name="bank", tag="bank")
+                nc.vector.tensor_scalar(out=pm[:, t, :], in0=gs_sb[:, k, t, cols(h)], scalar1=v_col[:, k, t : t + 1], scalar2=None, op0=ALU.mult)
+            tiles["pm", k, h] = pm
+
+        def pi(k, h, engine):
+            dst = quant_tile()
+            engine_copy(engine, mixed_out(dst[:]), mixed_in(tiles["pm", k, h][:]))
+            tiles["p", k, h] = dst
+
+        def pq(k, h):
+            quantise(tiles["p", k, h], "p", k, W * h)
+
+        def turn(which, g, k, engine):
+            dst = quant_tile()
+            d32 = dst[:].rearrange("p c t -> p (c t)").bitcast(F32).rearrange("p (c u) -> p c u", u=2)
+            src = tiles[which, g]
+            for half in range(2):
+                bank = psum.tile([P, 2, 2, P], F32, name="tbank", tag="tbank", bufs=2)
+                for i in range(2):
+                    w32 = src[:, 2 * half + i, :].bitcast(F32)
+                    for u in range(2):
+                        nc.tensor.transpose(bank[:, i, u, :], w32[:, 256 * k + u : 256 * (k + 1) : 2], ident[:])
+                engine_copy(
+                    engine,
+                    d32[:, 256 * half : 256 * half + 256, :].rearrange("p (i m) u -> p i m u", i=2),
+                    bank[:].rearrange("p i u m -> p i m u"),
+                )
+            tiles[which, g, k] = dst
+
+        def wq(which, g, k):
+            quantise(tiles[which, g, k], which, k, W * g)
+
+        def mm(which, g, h, pair):
+            lhs, rhs = {"1": ("g0", "p"), "2": ("gr", "q")}[which]
+            for t in (2 * pair, 2 * pair + 1):
+                acc = psum.tile([P, W], F32, name="bank", tag="bank", bufs=8 - 2)
                 m0 = W * g + P * t
                 for k in range(G):
                     nc.tensor.matmul_mx(
                         out=acc[:],
-                        lhsT=lc[:, k, m0 : m0 + P].bitcast(FP8X4),
-                        lhsT_scale=ls[:, k, m0 : m0 + P],
-                        rhs=rc[:, k, W * h : W * h + W].bitcast(FP8X4),
-                        rhs_scale=rs[:, k, W * h : W * h + W],
+                        lhsT=codes[lhs, k][:, m0 : m0 + P].bitcast(FP8X4),
+                        lhsT_scale=planes[lhs, k][:, m0 : m0 + P],
+                        rhs=codes[rhs, k][:, cols(h)].bitcast(FP8X4),
+                        rhs_scale=planes[rhs, k][:, cols(h)],
                         start=(k == 0),
                         stop=(k == G - 1),
                     )
-                banks.append(acc)
-            return banks
+                tiles["mm" + which, g, h, t] = acc
 
-        def make_u(banks, g, h):
-            u = work.tile([P, T, W], F32, name="u", tag="u", bufs=2)
-            for t in range(T):
-                nc.vector.tensor_tensor(
-                    out=u[:, t, :], in0=banks[t][:], in1=gs_sb[:, g, t, W * h : W * h + W], op=ALU.add
-                )
-            return u
+        def ug(g, h, pair):
+            if pair == 0:
+                tiles["u", g, h] = work.tile([P, T, W], F32, name="u", tag="u", bufs=2)
+            for t in (2 * pair + 1, 2 * pair):
+                nc.vector.tensor_tensor(out=tiles["u", g, h][:, t, :], in0=tiles["mm1", g, h, t][:], in1=gs_sb[:, g, t, cols(h)], op=ALU.add)
 
-        def make_q(u, g):
+        def uh(g, h):
             dst = quant_tile()
-            nc.vector.tensor_tensor(
-                out=dst[:],
-                in0=u[:].rearrange("p t s -> p s t"),
-                in1=dv_col[:, g, :].unsqueeze(1).to_broadcast([P, W, T]),
-                op=ALU.mult,
-            )
-            return dst
+            nc.vector.tensor_tensor(out=mixed_out(dst[:]), in0=mixed_in(tiles["u", g, h][:]), in1=spread(dv_col[:, g, :], W), op=ALU.mult)
+            tiles["q", g, h] = dst
 
-        lu = {}
-        ld = {}
-
-        def logs(g, h):
-            a = keep.tile([P, T, W], F32, name="lu%d%d" % (g, h))
-            b = keep.tile([P, T, W], F32, name="ld%d%d" % (g, h))
-            cols = slice(W * h, W * h + W)
-            nc.scalar.activation(out=a[:], in_=u0_sb[g][:, :, cols], func=ACT.Ln)
-            nc.scalar.activation(out=b[:], in_=do_sb[g][:, :, cols], func=ACT.Ln)
+        def dg(g, h, engine):
+            dst = work.tile([P, T, W], F32, name="dg", tag="dg", bufs=1)
             for t in range(T):
-                nc.gpsimd.tensor_tensor(out=b[:, t, :], in0=a[:, t, :], in1=b[:, t, :], op=ALU.subtract)
-            lu[g, h] = a
-            ld[g, h] = b
+                if engine == "S":
+                    nc.scalar.activation(out=dst[:, t, :], in_=gs_sb[:, g, t, cols(h)], func=ACT.Copy, scale=dv32[:, g, t : t + 1])
+                else:
+                    nc.vector.tensor_scalar(out=dst[:, t, :], in0=gs_sb[:, g, t, cols(h)], scalar1=dv32[:, g, t : t + 1], scalar2=None, op0=ALU.mult)
+            tiles["dg", g, h] = dst
 
-        def recip(g, h):
-            nc.scalar.activation(out=lu[g, h][:], in_=lu[g, h][:], func=ACT.Exp, scale=-1.0)
+        def sc(g, h, pair):
+            if pair == 0:
+                tiles["u", g, h] = work.tile([P, T, W], F32, name="u", tag="u", bufs=2)
+            for t in (2 * pair + 1, 2 * pair):
+                nc.scalar.activation(out=tiles["u", g, h][:, t, :], in_=tiles["mm1", g, h, t][:], func=ACT.Copy, scale=dv32[:, g, t : t + 1])
 
-        out_v = out.rearrange("(g p t) s -> g p t s", g=G, t=T)
-        o_s = [keep.tile([P, S], U8, name="o_s%d" % g, align_bytes=64) for g in range(G)]
+        def ua(g, h):
+            dst = quant_tile()
+            nc.vector.tensor_tensor(out=mixed_out(dst[:]), in0=mixed_in(tiles["u", g, h][:]), in1=mixed_in(tiles["dg", g, h][:]), op=ALU.add)
+            tiles["q", g, h] = dst
 
-        def phi(banks, g, h):
-            r = lu[g, h]
+        def qi(g, h, engine):
+            dst = quant_tile()
+            engine_copy(engine, mixed_out(dst[:]), mixed_in(tiles["qm", g, h][:]))
+            tiles["q", g, h] = dst
+
+        def us(g, h, engine):
+            qm = work.tile([P, T, W], BF16, name="pm", tag="pm", bufs=2)
             for t in range(T):
-                nc.vector.tensor_tensor(out=r[:, t, :], in0=banks[t][:], in1=r[:, t, :], op=ALU.mult)
+                if engine == "V":
+                    nc.vector.tensor_scalar(out=qm[:, t, :], in0=tiles["u", g, h][:, t, :], scalar1=dv32[:, g, t : t + 1], scalar2=None, op0=ALU.mult)
+                    continue
+                nc.scalar.activation(out=qm[:, t, :], in_=tiles["u", g, h][:, t, :], func=ACT.Copy, scale=dv32[:, g, t : t + 1])
+            tiles["qm", g, h] = qm
 
-        def finish(g, h, c0, cn):
-            r = lu[g, h]
-            cols = slice(c0, c0 + cn)
-            nc.vector.tensor_tensor(out=r[:, :, cols], in0=r[:, :, cols], in1=ld[g, h][:, :, cols], op=ALU.add)
-            nc.sync.dma_start(out=out_v[g, :, :, W * h + c0 : W * h + c0 + cn], in_=r[:, :, cols])
+        def qq(g, h):
+            quantise(tiles["q", g, h], "q", g, W * h)
 
-        def round_out(dst, g, h, c0, cn, engine):
-            view = lu[g, h][:, :, c0 : c0 + cn].rearrange("p t s -> p s t")
-            if engine == "scalar":
-                nc.scalar.copy(out=dst[:, c0 : c0 + cn, :], in_=view)
+        def lead():
+            first = keep.tile([P, W], BF16, name="first")
+            nc.sync.dma_start(out=first[:], in_=u0.rearrange("(g p t) c -> g p t c", g=G, t=T)[0, :, 0, 0:W])
+            tiles["lnu0", 0, 0] = keep.tile([P, T, W], F32, name="lnu000")
+            nc.scalar.activation(out=tiles["lnu0", 0, 0][:, 0, :], in_=first[:], func=ACT.Ln)
+
+        def ln(which, g, h):
+            if (which, g, h) == ("u0", 0, 0):
+                nc.scalar.activation(out=tiles["lnu0", 0, 0][:, 1:T, :], in_=tiles[which, g][:, 1:T, cols(h)], func=ACT.Ln)
+                return
+            dst = keep.tile([P, T, W], F32, name="ln" + which + str(g) + str(h))
+            nc.scalar.activation(out=dst[:], in_=tiles[which, g][:, :, cols(h)], func=ACT.Ln)
+            tiles["ln" + which, g, h] = dst
+
+        def df(g, h, t0, engine):
+            a, b = tiles["lnu0", g, h], tiles["lndo", g, h]
+            if engine == "V":
+                c = slice(t0, t0 + 2)
+                nc.vector.tensor_tensor(out=b[:, c, :], in0=a[:, c, :], in1=b[:, c, :], op=ALU.subtract)
             else:
-                nc.vector.tensor_copy(out=dst[:, c0 : c0 + cn, :], in_=view)
+                for t in range(t0, t0 + 2):
+                    nc.gpsimd.tensor_tensor(out=b[:, t, :], in0=a[:, t, :], in1=b[:, t, :], op=ALU.subtract)
 
-        def store_planes(src, g, h, c0, cn):
-            codes = work.tile([P, W], U32, name="o_c", tag="o_c", bufs=2, align_bytes=64)
+        def rx(g, h):
+            a = tiles["lnu0", g, h]
+            nc.scalar.activation(out=a[:], in_=a[:], func=ACT.Exp, scale=-1.0)
+
+        def om(g, h, pair):
+            r = tiles["lnu0", g, h]
+            for t in (2 * pair + 1, 2 * pair):
+                nc.vector.tensor_tensor(out=r[:, t, :], in0=tiles["mm2", g, h, t][:], in1=r[:, t, :], op=ALU.mult)
+
+        def pf(g, h, c0, cn, engine):
+            r = tiles["lnu0", g, h]
+            c = slice(c0, c0 + cn)
+            if engine == "V":
+                nc.vector.tensor_tensor(out=r[:, :, c], in0=r[:, :, c], in1=tiles["lndo", g, h][:, :, c], op=ALU.add)
+            else:
+                for c1 in range(c0, c0 + cn, 128):
+                    d = slice(c1, c1 + 128)
+                    nc.gpsimd.tensor_tensor(out=r[:, :, d], in0=r[:, :, d], in1=tiles["lndo", g, h][:, :, d], op=ALU.add)
+            nc.sync.dma_start(out=out_v[g, :, :, W * h + c0 : W * h + c0 + cn], in_=r[:, :, c])
+
+        def oc(g, h, c0, cn, engine):
+            if ("ob", g, h) not in tiles:
+                tiles["ob", g, h] = quant_tile()
+            dst = tiles["ob", g, h]
+            engine_copy(engine, mixed_out(dst[:, c0 : c0 + cn, :]), mixed_in(tiles["lnu0", g, h][:, :, c0 : c0 + cn]))
+
+        def oq(g, h, c0, cn):
+            dst = work.tile([P, W], U32, name="o_c", tag="o_c", bufs=4, align_bytes=64)
             s0 = W * h + c0
             nc.vector.quantize_mx(
-                out=codes[:, c0 : c0 + cn].bitcast(FP8X4),
-                scales=o_s[g][:, s0 : s0 + cn],
-                in_=src[:, c0 : c0 + cn, :].rearrange("p c t -> p (c t)"),
+                out=dst[:, c0 : c0 + cn].bitcast(FP8X4),
+                scales=planes["o", g][:, s0 : s0 + cn],
+                in_=tiles["ob", g, h][:, c0 : c0 + cn, :].rearrange("p c t -> p (c t)"),
             )
             nc.sync.dma_start(
                 out=words[g, :, s0 : s0 + cn, :].rearrange("p m t -> p (m t)").bitcast(I32),
-                in_=codes[:, c0 : c0 + cn].bitcast(I32),
+                in_=dst[:, c0 : c0 + cn].bitcast(I32),
             )
 
         def store_scales(g):
             for q in range(4):
                 nc.sync.dma_start(
                     out=scales[g, 4 * q : 4 * q + 4, :].bitcast(I32),
-                    in_=o_s[g][32 * q : 32 * q + 4, :].bitcast(I32),
+                    in_=planes["o", g][32 * q : 32 * q + 4, :].bitcast(I32),
                 )
 
-        pa = [make_p(0, 0), make_p(1, 0)]
-        for k in range(G):
-            quantise(pa[k], p_c, p_s, k, 0)
-        xa = turn_group(g0_sb[0])
-        for k in range(G):
-            quantise(xa[k], g0_c, g0_s, k, 0)
-        t0 = product(g0_c, g0_s, p_c, p_s, 0, 0)
-        pb = [make_p(0, 1), make_p(1, 1)]
-        xb = turn_group(g0_sb[1])
-        for k in range(G):
-            quantise(xb[k], g0_c, g0_s, k, W)
-        t1 = product(g0_c, g0_s, p_c, p_s, 1, 0)
-        u_0 = make_u(t0, 0, 0)
-        for k in range(G):
-            quantise(pb[k], p_c, p_s, k, W)
-        t2 = product(g0_c, g0_s, p_c, p_s, 0, 1)
-        u_1 = make_u(t1, 1, 0)
-        logs(0, 0)
-        logs(0, 1)
-        qa = make_q(u_0, 0)
-        u_2 = make_u(t2, 0, 1)
-        quantise(qa, q_c, q_s, 0, 0)
-        t3 = product(g0_c, g0_s, p_c, p_s, 1, 1)
-        qb = make_q(u_1, 1)
-        u_3 = make_u(t3, 1, 1)
-        quantise(qb, q_c, q_s, 1, 0)
-        ya = turn_group(gr_sb[0])
-        qc = make_q(u_2, 0)
-        for k in range(G):
-            quantise(ya[k], gr_c, gr_s, k, 0)
-        quantise(qc, q_c, q_s, 0, W)
-        yb = turn_group(gr_sb[1])
-        qd = make_q(u_3, 1)
-        for k in range(G):
-            quantise(yb[k], gr_c, gr_s, k, W)
-        quantise(qd, q_c, q_s, 1, W)
-        logs(1, 0)
-        logs(1, 1)
-        order = [(0, 0), (0, 1), (1, 0), (1, 1)]
-        for g, h in order:
-            recip(g, h)
-
-        acc = {}
-        acc[0] = product(gr_c, gr_s, q_c, q_s, 0, 0)
-        phi(acc[0], 0, 0)
-        acc[1] = product(gr_c, gr_s, q_c, q_s, 0, 1)
-        phi(acc[1], 0, 1)
-        rounded = {}
-        for i in range(4):
-            g, h = order[i]
-            rounded[i] = quant_tile()
-            if i < 3:
-                finish(g, h, 0, W)
-                round_out(rounded[i], g, h, 0, W, "scalar")
-            else:
-                finish(g, h, 0, W // 2)
-                round_out(rounded[i], g, h, 0, W // 2, "scalar")
-                finish(g, h, W // 2, W // 2)
-                round_out(rounded[i], g, h, W // 2, W // 2, "vector")
-            if i + 2 < 4:
-                acc[i + 2] = product(gr_c, gr_s, q_c, q_s, order[i + 2][0], order[i + 2][1])
-                phi(acc[i + 2], order[i + 2][0], order[i + 2][1])
-            if i > 0:
-                pg, ph = order[i - 1]
-                store_planes(rounded[i - 1], pg, ph, 0, W)
-                if ph == 1:
-                    store_scales(pg)
-        store_planes(rounded[3], 1, 1, 0, W // 2)
-        store_planes(rounded[3], 1, 1, W // 2, W // 2)
-        store_scales(1)
+        steps = {"lead": lead, "dv": load_dv, "Lgs": load_gs, "L": load, "pt": pt, "ps": ps, "pi": pi, "pq": pq, "turn": turn, "wq": wq, "mm": mm, "ug": ug, "uh": uh,
+                 "dg": dg, "sc": sc, "ua": ua, "us": us, "qi": qi, "qq": qq, "ln": ln, "df": df, "rx": rx, "om": om, "pf": pf, "oc": oc, "oq": oq, "os": store_scales}
+        for step in ORDER:
+            steps[step[0]](*step[1:])

@@ -21,127 +21,125 @@ G = 2
 H = 2
 W = 512
 ORDER = [
-    ("Lgs", 1, 0),
-    ("ps", 1, 0),
+    ("Lgs", 1, 0, 0, 1024),
     ("lead",),
-    ("dv",),
-    ("Lgs", 0, 0, 0, 256),
-    ("Lgs", 0, 0, 256, 256),
-    ("Lgs", 0, 1),
+    ("ps", 1, 0),
     ("L", "g0", 0),
-    ("pt", 0, 0, 0, 256),
-    ("ps", 0, 1),
-    ("pi", 0, 1, "S"),
     ("turn", "g0", 0, 1, "S"),
-    ("L", "u0", 0),
-    ("L", "g0", 1),
+    ("ps", 1, 1),
+    ("pi", 1, 1, "V"),
     ("pi", 1, 0, "V"),
-    ("Lgs", 1, 1),
-    ("ln", "u0", 0, 1),
-    ("pt", 0, 0, 256, 256),
+    ("L", "u0", 0),
+    ("wq", "g0", 0, 1),
     ("ln", "u0", 0, 0),
     ("pq", 1, 0),
-    ("pq", 0, 0),
-    ("pq", 0, 1),
-    ("wq", "g0", 0, 1),
-    ("turn", "g0", 0, 0, "V"),
-    ("L", "do", 0),
-    ("wq", "g0", 0, 0),
+    ("turn", "g0", 0, 0, "S"),
+    ("Lgs", 0, 0, 0, 1024),
+    ("ln", "u0", 0, 1),
+    ("ps", 0, 1),
+    ("ps", 0, 0),
+    ("pi", 0, 0, "V"),
+    ("L", "g0", 1),
     ("turn", "g0", 1, 0, "S"),
-    ("L", "u0", 1),
+    ("wq", "g0", 0, 0),
+    ("L", "do", 0),
     ("ln", "do", 0, 0),
-    ("pt", 1, 1),
-    ("df", 0, 0, 2, "G"),
+    ("pq", 0, 0),
+    ("pi", 0, 1, "V"),
+    ("pq", 1, 1),
     ("mm", "1", 0, 0, 0),
     ("wq", "g0", 1, 0),
+    ("pq", 0, 1),
     ("turn", "g0", 1, 1, "S"),
-    ("L", "do", 1),
-    ("mm", "1", 0, 0, 1),
-    ("pq", 1, 1),
-    ("mm", "1", 0, 1, 0),
-    ("ug", 0, 0, 0),
-    ("ug", 0, 0, 1),
-    ("L", "gr", 1),
-    ("mm", "1", 0, 1, 1),
+    ("L", "u0", 1),
     ("ln", "do", 0, 1),
-    ("wq", "g0", 1, 1),
+    ("dv",),
+    ("L", "do", 1),
     ("ln", "do", 1, 1),
-    ("df", 0, 1, 0, "G"),
-    ("mm", "1", 1, 0, 0),
-    ("df", 0, 1, 2, "G"),
-    ("uh", 0, 0),
-    ("ug", 0, 1, 0),
-    ("mm", "1", 1, 0, 1),
-    ("ug", 0, 1, 1),
-    ("ln", "do", 1, 0),
-    ("us", 0, 1, "S"),
-    ("mm", "1", 1, 1, 1),
-    ("ug", 1, 0, 0),
-    ("L", "gr", 0),
-    ("mm", "1", 1, 1, 0),
-    ("ug", 1, 0, 1),
-    ("ug", 1, 1, 0),
+    ("ug", 0, 0, 0),
+    ("mm", "1", 0, 0, 1),
     ("ln", "u0", 1, 1),
-    ("turn", "gr", 1, 1, "V"),
+    ("df", 0, 0, 2, "G"),
+    ("wq", "g0", 1, 1),
+    ("df", 0, 1, 0, "G"),
+    ("mm", "1", 0, 1, 0),
+    ("ug", 0, 0, 1),
+    ("L", "gr", 0),
+    ("ug", 0, 1, 0),
+    ("uh", 0, 0),
+    ("mm", "1", 0, 1, 1),
+    ("mm", "1", 1, 1, 0),
+    ("ug", 0, 1, 1),
+    ("df", 0, 1, 2, "G"),
+    ("mm", "1", 1, 1, 1),
+    ("us", 0, 1, "S"),
+    ("df", 0, 0, 0, "V"),
+    ("turn", "gr", 0, 0, "V"),
+    ("mm", "1", 1, 0, 0),
+    ("ug", 1, 0, 0),
+    ("ug", 1, 1, 0),
+    ("L", "gr", 1),
     ("ln", "u0", 1, 0),
-    ("df", 0, 0, 0, "G"),
-    ("qi", 0, 1, "V"),
-    ("ug", 1, 1, 1),
-    ("qq", 0, 1),
-    ("turn", "gr", 0, 1, "S"),
-    ("us", 1, 0, "S"),
+    ("df", 1, 1, 2, "V"),
+    ("turn", "gr", 1, 1, "V"),
+    ("ln", "do", 1, 0),
+    ("qi", 0, 1, "S"),
+    ("mm", "1", 1, 0, 1),
     ("df", 1, 1, 0, "G"),
+    ("turn", "gr", 0, 1, "S"),
+    ("df", 1, 0, 0, "G"),
+    ("ug", 1, 0, 1),
+    ("ug", 1, 1, 1),
+    ("us", 1, 1, "V"),
     ("wq", "gr", 0, 1),
     ("turn", "gr", 1, 0, "S"),
-    ("qi", 1, 0, "S"),
-    ("us", 1, 1, "V"),
-    ("turn", "gr", 0, 0, "S"),
-    ("df", 1, 0, 2, "V"),
-    ("rx", 0, 0),
-    ("df", 1, 0, 0, "V"),
+    ("us", 1, 0, "V"),
+    ("qq", 0, 1),
     ("qq", 0, 0),
-    ("wq", "gr", 1, 0),
-    ("qq", 1, 0),
+    ("qi", 1, 1, "S"),
+    ("qi", 1, 0, "V"),
     ("wq", "gr", 0, 0),
-    ("rx", 0, 1),
-    ("mm", "2", 0, 0, 1),
-    ("df", 1, 1, 2, "V"),
-    ("qi", 1, 1, "V"),
-    ("rx", 1, 1),
+    ("qq", 1, 0),
     ("mm", "2", 0, 0, 0),
+    ("mm", "2", 0, 0, 1),
+    ("df", 1, 0, 2, "V"),
+    ("qq", 1, 1),
+    ("rx", 0, 0),
+    ("rx", 0, 1),
     ("wq", "gr", 1, 1),
     ("rx", 1, 0),
-    ("qq", 1, 1),
     ("om", 0, 0, 0),
+    ("mm", "2", 0, 1, 0),
     ("mm", "2", 0, 1, 1),
     ("om", 0, 0, 1),
-    ("mm", "2", 0, 1, 0),
-    ("mm", "2", 1, 0, 0),
-    ("om", 0, 1, 1),
-    ("om", 0, 1, 0),
-    ("pf", 0, 0, 0, 512, "V"),
-    ("mm", "2", 1, 1, 1),
+    ("pf", 0, 0, 0, 512, "G"),
+    ("wq", "gr", 1, 0),
     ("mm", "2", 1, 0, 1),
-    ("om", 1, 0, 0),
-    ("mm", "2", 1, 1, 0),
+    ("om", 0, 1, 0),
+    ("mm", "2", 1, 1, 1),
+    ("om", 0, 1, 1),
+    ("mm", "2", 1, 0, 0),
     ("om", 1, 0, 1),
-    ("pf", 0, 1, 0, 512, "G"),
-    ("om", 1, 1, 1),
-    ("om", 1, 1, 0),
+    ("rx", 1, 1),
+    ("om", 1, 0, 0),
+    ("pf", 0, 1, 0, 512, "V"),
     ("pf", 1, 0, 0, 512, "V"),
+    ("mm", "2", 1, 1, 0),
+    ("om", 1, 1, 0),
+    ("om", 1, 1, 1),
     ("oc", 0, 0, 0, 512, "S"),
-    ("pf", 1, 1, 0, 256, "V"),
-    ("oc", 0, 1, 0, 512, "S"),
-    ("oq", 0, 1, 0, 512),
-    ("pf", 1, 1, 256, 256, "V"),
-    ("oc", 1, 1, 0, 256, "S"),
-    ("oc", 1, 1, 256, 256, "S"),
     ("oq", 0, 0, 0, 512),
-    ("oc", 1, 0, 0, 512, "V"),
-    ("os", 0),
-    ("oq", 1, 1, 256, 256),
+    ("oc", 1, 0, 0, 512, "S"),
+    ("pf", 1, 1, 256, 256, "V"),
+    ("pf", 1, 1, 0, 256, "V"),
     ("oq", 1, 0, 0, 512),
+    ("oc", 0, 1, 0, 512, "S"),
+    ("oc", 1, 1, 0, 256, "V"),
+    ("oq", 0, 1, 0, 512),
+    ("oc", 1, 1, 256, 256, "S"),
     ("oq", 1, 1, 0, 256),
+    ("oq", 1, 1, 256, 256),
+    ("os", 0),
     ("os", 1),
 ]
 

from contextlib import ExitStack

import concourse.mybir as mybir
from concourse.masks import make_identity

N, S, R = 1024, 1024, 1024
FLOPS = 2 * N * N * S + 2 * R * N * S

F32 = mybir.dt.float32
BF16 = mybir.dt.bfloat16
U32 = mybir.dt.uint32
I32 = mybir.dt.int32
U8 = mybir.dt.uint8
FP8X4 = mybir.dt.float8_e4m3fn_x4
ALU = mybir.AluOpType
ACT = mybir.ActivationFunctionType

P = 128
T = 4
G = 2
H = 2
W = 512
ORDER = [
    ("Lgs", 1, 0, 0, 1024),
    ("lead",),
    ("ps", 1, 0),
    ("L", "g0", 0),
    ("turn", "g0", 0, 1, "S"),
    ("ps", 1, 1),
    ("pi", 1, 1, "V"),
    ("pi", 1, 0, "V"),
    ("L", "u0", 0),
    ("wq", "g0", 0, 1),
    ("ln", "u0", 0, 0),
    ("pq", 1, 0),
    ("turn", "g0", 0, 0, "S"),
    ("Lgs", 0, 0, 0, 1024),
    ("ln", "u0", 0, 1),
    ("ps", 0, 1),
    ("ps", 0, 0),
    ("pi", 0, 0, "V"),
    ("L", "g0", 1),
    ("turn", "g0", 1, 0, "S"),
    ("wq", "g0", 0, 0),
    ("L", "do", 0),
    ("ln", "do", 0, 0),
    ("pq", 0, 0),
    ("pi", 0, 1, "V"),
    ("pq", 1, 1),
    ("mm", "1", 0, 0, 0),
    ("wq", "g0", 1, 0),
    ("pq", 0, 1),
    ("turn", "g0", 1, 1, "S"),
    ("L", "u0", 1),
    ("ln", "do", 0, 1),
    ("dv",),
    ("L", "do", 1),
    ("ln", "do", 1, 1),
    ("ug", 0, 0, 0),
    ("mm", "1", 0, 0, 1),
    ("ln", "u0", 1, 1),
    ("df", 0, 0, 2, "G"),
    ("wq", "g0", 1, 1),
    ("df", 0, 1, 0, "G"),
    ("mm", "1", 0, 1, 0),
    ("ug", 0, 0, 1),
    ("L", "gr", 0),
    ("ug", 0, 1, 0),
    ("uh", 0, 0),
    ("mm", "1", 0, 1, 1),
    ("mm", "1", 1, 1, 0),
    ("ug", 0, 1, 1),
    ("df", 0, 1, 2, "G"),
    ("mm", "1", 1, 1, 1),
    ("us", 0, 1, "S"),
    ("df", 0, 0, 0, "V"),
    ("turn", "gr", 0, 0, "V"),
    ("mm", "1", 1, 0, 0),
    ("ug", 1, 0, 0),
    ("ug", 1, 1, 0),
    ("L", "gr", 1),
    ("ln", "u0", 1, 0),
    ("df", 1, 1, 2, "V"),
    ("turn", "gr", 1, 1, "V"),
    ("ln", "do", 1, 0),
    ("qi", 0, 1, "S"),
    ("mm", "1", 1, 0, 1),
    ("df", 1, 1, 0, "G"),
    ("turn", "gr", 0, 1, "S"),
    ("df", 1, 0, 0, "G"),
    ("ug", 1, 0, 1),
    ("ug", 1, 1, 1),
    ("us", 1, 1, "V"),
    ("wq", "gr", 0, 1),
    ("turn", "gr", 1, 0, "S"),
    ("us", 1, 0, "V"),
    ("qq", 0, 1),
    ("qq", 0, 0),
    ("qi", 1, 1, "S"),
    ("qi", 1, 0, "V"),
    ("wq", "gr", 0, 0),
    ("qq", 1, 0),
    ("mm", "2", 0, 0, 0),
    ("mm", "2", 0, 0, 1),
    ("df", 1, 0, 2, "V"),
    ("qq", 1, 1),
    ("rx", 0, 0),
    ("rx", 0, 1),
    ("wq", "gr", 1, 1),
    ("rx", 1, 0),
    ("om", 0, 0, 0),
    ("mm", "2", 0, 1, 0),
    ("mm", "2", 0, 1, 1),
    ("om", 0, 0, 1),
    ("pf", 0, 0, 0, 512, "G"),
    ("wq", "gr", 1, 0),
    ("mm", "2", 1, 0, 1),
    ("om", 0, 1, 0),
    ("mm", "2", 1, 1, 1),
    ("om", 0, 1, 1),
    ("mm", "2", 1, 0, 0),
    ("om", 1, 0, 1),
    ("rx", 1, 1),
    ("om", 1, 0, 0),
    ("pf", 0, 1, 0, 512, "V"),
    ("pf", 1, 0, 0, 512, "V"),
    ("mm", "2", 1, 1, 0),
    ("om", 1, 1, 0),
    ("om", 1, 1, 1),
    ("oc", 0, 0, 0, 512, "S"),
    ("oq", 0, 0, 0, 512),
    ("oc", 1, 0, 0, 512, "S"),
    ("pf", 1, 1, 256, 256, "V"),
    ("pf", 1, 1, 0, 256, "V"),
    ("oq", 1, 0, 0, 512),
    ("oc", 0, 1, 0, 512, "S"),
    ("oc", 1, 1, 0, 256, "V"),
    ("oq", 0, 1, 0, 512),
    ("oc", 1, 1, 256, 256, "S"),
    ("oq", 1, 1, 0, 256),
    ("oq", 1, 1, 256, 256),
    ("os", 0),
    ("os", 1),
]


def tile_laplacedomaindistortedbornrytovresidual_x1_kernel(tc, gs, g0, gr, v, dv, u0, dobs, out, words, scales):
    nc = tc.nc
    with ExitStack() as ctx:
        keep = ctx.enter_context(tc.tile_pool(name="keep", bufs=1))
        work = ctx.enter_context(tc.tile_pool(name="work", bufs=2))
        psum = ctx.enter_context(tc.psum_pool(name="psum", bufs=2))
        ctx.enter_context(tc.manual_schedule())
        tiles = {}

        v_col = keep.tile([P, G, T], BF16, name="v_col")
        dv_col = keep.tile([P, G, T], BF16, name="dv_col")
        nc.scalar.dma_start(out=v_col[:], in_=v.rearrange("(g p t) -> p g t", g=G, t=T))
        dv32 = keep.tile([P, G, T], F32, name="dv32")
        ident = keep.tile([P, P], F32, name="ident")
        make_identity(nc, ident[:])

        gs_sb = keep.tile([P, G, T, S], BF16, name="gs_sb")
        gs_v = gs.rearrange("(g p t) s -> g p t s", g=G, t=T)
        out_v = out.rearrange("(g p t) s -> g p t s", g=G, t=T)

        def cols(h):
            return slice(W * h, W * h + W)

        def load_gs(g, h, c0=0, cn=W):
            c = slice(W * h + c0, W * h + c0 + cn)
            nc.sync.dma_start(out=gs_sb[:, g, :, c], in_=gs_v[g, :, :, c])

        def load_dv():
            nc.sync.dma_start(out=dv_col[:], in_=dv.rearrange("(g p t) -> p g t", g=G, t=T))
            nc.gpsimd.tensor_copy(out=dv32[:], in_=dv_col[:])

        def load(which, g):
            src = {"g0": g0, "gr": gr, "u0": u0, "do": dobs}[which]
            if which.startswith("g"):
                tile = work.tile([P, T, 1024], BF16, name="wraw", tag="wraw", bufs=2)
            else:
                tile = keep.tile([P, T, 1024], BF16, name=which + str(g))
            nc.sync.dma_start(out=tile[:], in_=src.rearrange("(g p t) c -> g p t c", g=G, t=T)[g])
            tiles[which, g] = tile

        codes = {}
        planes = {}
        for which in ["p", "q", "g0", "gr"]:
            for k in range(G):
                codes[which, k] = keep.tile([P, 1024], U32, name=which + "_c" + str(k), align_bytes=64)
                planes[which, k] = keep.tile([P, 1024], U8, name=which + "_s" + str(k), align_bytes=64)
        for g in range(G):
            planes["o", g] = keep.tile([P, S], U8, name="o_s" + str(g), align_bytes=64)

        def quant_tile():
            return work.tile([P, W, T], BF16, name="qin", tag="qin", bufs=8, align_bytes=64)

        def quantise(src, which, k, c0):
            nc.vector.quantize_mx(
                out=codes[which, k][:, c0 : c0 + W].bitcast(FP8X4),
                scales=planes[which, k][:, c0 : c0 + W],
                in_=src[:].rearrange("p c t -> p (c t)"),
            )

        def mixed_in(ap):
            return ap.rearrange("p t (c i) -> p c t i", i=4)

        def mixed_out(ap):
            return ap.rearrange("p (c i) t -> p c t i", i=4)

        def spread(col, n):
            return col.unsqueeze(1).unsqueeze(3).to_broadcast([P, n // 4, T, 4])

        def engine_copy(engine, out, in_):
            if engine == "S":
                nc.scalar.copy(out=out, in_=in_)
            elif engine == "V":
                nc.vector.tensor_copy(out=out, in_=in_)
            else:
                nc.gpsimd.tensor_scalar(out=out, in0=in_, scalar1=1.0, scalar2=0.0, op0=ALU.mult, op1=ALU.add)

        def pt(k, h, c0=0, cn=W):
            if ("p", k, h) not in tiles:
                tiles["p", k, h] = quant_tile()
            c = slice(W * h + c0, W * h + c0 + cn)
            nc.vector.tensor_tensor(
                out=mixed_out(tiles["p", k, h][:, c0 : c0 + cn, :]), in0=mixed_in(gs_sb[:, k, :, c]), in1=spread(v_col[:, k, :], cn), op=ALU.mult
            )

        def ps(k, h):
            pm = work.tile([P, T, W], BF16, name="pm", tag="pm", bufs=2)
            for t in range(T):
                nc.vector.tensor_scalar(out=pm[:, t, :], in0=gs_sb[:, k, t, cols(h)], scalar1=v_col[:, k, t : t + 1], scalar2=None, op0=ALU.mult)
            tiles["pm", k, h] = pm

        def pi(k, h, engine):
            dst = quant_tile()
            engine_copy(engine, mixed_out(dst[:]), mixed_in(tiles["pm", k, h][:]))
            tiles["p", k, h] = dst

        def pq(k, h):
            quantise(tiles["p", k, h], "p", k, W * h)

        def turn(which, g, k, engine):
            dst = quant_tile()
            d32 = dst[:].rearrange("p c t -> p (c t)").bitcast(F32).rearrange("p (c u) -> p c u", u=2)
            src = tiles[which, g]
            for half in range(2):
                bank = psum.tile([P, 2, 2, P], F32, name="tbank", tag="tbank", bufs=2)
                for i in range(2):
                    w32 = src[:, 2 * half + i, :].bitcast(F32)
                    for u in range(2):
                        nc.tensor.transpose(bank[:, i, u, :], w32[:, 256 * k + u : 256 * (k + 1) : 2], ident[:])
                engine_copy(
                    engine,
                    d32[:, 256 * half : 256 * half + 256, :].rearrange("p (i m) u -> p i m u", i=2),
                    bank[:].rearrange("p i u m -> p i m u"),
                )
            tiles[which, g, k] = dst

        def wq(which, g, k):
            quantise(tiles[which, g, k], which, k, W * g)

        def mm(which, g, h, pair):
            lhs, rhs = {"1": ("g0", "p"), "2": ("gr", "q")}[which]
            for t in (2 * pair, 2 * pair + 1):
                acc = psum.tile([P, W], F32, name="bank", tag="bank", bufs=8 - 2)
                m0 = W * g + P * t
                for k in range(G):
                    nc.tensor.matmul_mx(
                        out=acc[:],
                        lhsT=codes[lhs, k][:, m0 : m0 + P].bitcast(FP8X4),
                        lhsT_scale=planes[lhs, k][:, m0 : m0 + P],
                        rhs=codes[rhs, k][:, cols(h)].bitcast(FP8X4),
                        rhs_scale=planes[rhs, k][:, cols(h)],
                        start=(k == 0),
                        stop=(k == G - 1),
                    )
                tiles["mm" + which, g, h, t] = acc

        def ug(g, h, pair):
            if pair == 0:
                tiles["u", g, h] = work.tile([P, T, W], F32, name="u", tag="u", bufs=2)
            for t in (2 * pair + 1, 2 * pair):
                nc.vector.tensor_tensor(out=tiles["u", g, h][:, t, :], in0=tiles["mm1", g, h, t][:], in1=gs_sb[:, g, t, cols(h)], op=ALU.add)

        def uh(g, h):
            dst = quant_tile()
            nc.vector.tensor_tensor(out=mixed_out(dst[:]), in0=mixed_in(tiles["u", g, h][:]), in1=spread(dv_col[:, g, :], W), op=ALU.mult)
            tiles["q", g, h] = dst

        def dg(g, h, engine):
            dst = work.tile([P, T, W], F32, name="dg", tag="dg", bufs=1)
            for t in range(T):
                if engine == "S":
                    nc.scalar.activation(out=dst[:, t, :], in_=gs_sb[:, g, t, cols(h)], func=ACT.Copy, scale=dv32[:, g, t : t + 1])
                else:
                    nc.vector.tensor_scalar(out=dst[:, t, :], in0=gs_sb[:, g, t, cols(h)], scalar1=dv32[:, g, t : t + 1], scalar2=None, op0=ALU.mult)
            tiles["dg", g, h] = dst

        def sc(g, h, pair):
            if pair == 0:
                tiles["u", g, h] = work.tile([P, T, W], F32, name="u", tag="u", bufs=2)
            for t in (2 * pair + 1, 2 * pair):
                nc.scalar.activation(out=tiles["u", g, h][:, t, :], in_=tiles["mm1", g, h, t][:], func=ACT.Copy, scale=dv32[:, g, t : t + 1])

        def ua(g, h):
            dst = quant_tile()
            nc.vector.tensor_tensor(out=mixed_out(dst[:]), in0=mixed_in(tiles["u", g, h][:]), in1=mixed_in(tiles["dg", g, h][:]), op=ALU.add)
            tiles["q", g, h] = dst

        def qi(g, h, engine):
            dst = quant_tile()
            engine_copy(engine, mixed_out(dst[:]), mixed_in(tiles["qm", g, h][:]))
            tiles["q", g, h] = dst

        def us(g, h, engine):
            qm = work.tile([P, T, W], BF16, name="pm", tag="pm", bufs=2)
            for t in range(T):
                if engine == "V":
                    nc.vector.tensor_scalar(out=qm[:, t, :], in0=tiles["u", g, h][:, t, :], scalar1=dv32[:, g, t : t + 1], scalar2=None, op0=ALU.mult)
                    continue
                nc.scalar.activation(out=qm[:, t, :], in_=tiles["u", g, h][:, t, :], func=ACT.Copy, scale=dv32[:, g, t : t + 1])
            tiles["qm", g, h] = qm

        def qq(g, h):
            quantise(tiles["q", g, h], "q", g, W * h)

        def lead():
            first = keep.tile([P, W], BF16, name="first")
            nc.sync.dma_start(out=first[:], in_=u0.rearrange("(g p t) c -> g p t c", g=G, t=T)[0, :, 0, 0:W])
            tiles["lnu0", 0, 0] = keep.tile([P, T, W], F32, name="lnu000")
            nc.scalar.activation(out=tiles["lnu0", 0, 0][:, 0, :], in_=first[:], func=ACT.Ln)

        def ln(which, g, h):
            if (which, g, h) == ("u0", 0, 0):
                nc.scalar.activation(out=tiles["lnu0", 0, 0][:, 1:T, :], in_=tiles[which, g][:, 1:T, cols(h)], func=ACT.Ln)
                return
            dst = keep.tile([P, T, W], F32, name="ln" + which + str(g) + str(h))
            nc.scalar.activation(out=dst[:], in_=tiles[which, g][:, :, cols(h)], func=ACT.Ln)
            tiles["ln" + which, g, h] = dst

        def df(g, h, t0, engine):
            a, b = tiles["lnu0", g, h], tiles["lndo", g, h]
            if engine == "V":
                c = slice(t0, t0 + 2)
                nc.vector.tensor_tensor(out=b[:, c, :], in0=a[:, c, :], in1=b[:, c, :], op=ALU.subtract)
            else:
                for t in range(t0, t0 + 2):
                    nc.gpsimd.tensor_tensor(out=b[:, t, :], in0=a[:, t, :], in1=b[:, t, :], op=ALU.subtract)

        def rx(g, h):
            a = tiles["lnu0", g, h]
            nc.scalar.activation(out=a[:], in_=a[:], func=ACT.Exp, scale=-1.0)

        def om(g, h, pair):
            r = tiles["lnu0", g, h]
            for t in (2 * pair + 1, 2 * pair):
                nc.vector.tensor_tensor(out=r[:, t, :], in0=tiles["mm2", g, h, t][:], in1=r[:, t, :], op=ALU.mult)

        def pf(g, h, c0, cn, engine):
            r = tiles["lnu0", g, h]
            c = slice(c0, c0 + cn)
            if engine == "V":
                nc.vector.tensor_tensor(out=r[:, :, c], in0=r[:, :, c], in1=tiles["lndo", g, h][:, :, c], op=ALU.add)
            else:
                for c1 in range(c0, c0 + cn, 128):
                    d = slice(c1, c1 + 128)
                    nc.gpsimd.tensor_tensor(out=r[:, :, d], in0=r[:, :, d], in1=tiles["lndo", g, h][:, :, d], op=ALU.add)
            nc.sync.dma_start(out=out_v[g, :, :, W * h + c0 : W * h + c0 + cn], in_=r[:, :, c])

        def oc(g, h, c0, cn, engine):
            if ("ob", g, h) not in tiles:
                tiles["ob", g, h] = quant_tile()
            dst = tiles["ob", g, h]
            engine_copy(engine, mixed_out(dst[:, c0 : c0 + cn, :]), mixed_in(tiles["lnu0", g, h][:, :, c0 : c0 + cn]))

        def oq(g, h, c0, cn):
            dst = work.tile([P, W], U32, name="o_c", tag="o_c", bufs=4, align_bytes=64)
            s0 = W * h + c0
            nc.vector.quantize_mx(
                out=dst[:, c0 : c0 + cn].bitcast(FP8X4),
                scales=planes["o", g][:, s0 : s0 + cn],
                in_=tiles["ob", g, h][:, c0 : c0 + cn, :].rearrange("p c t -> p (c t)"),
            )
            nc.sync.dma_start(
                out=words[g, :, s0 : s0 + cn, :].rearrange("p m t -> p (m t)").bitcast(I32),
                in_=dst[:, c0 : c0 + cn].bitcast(I32),
            )

        def store_scales(g):
            for q in range(4):
                nc.sync.dma_start(
                    out=scales[g, 4 * q : 4 * q + 4, :].bitcast(I32),
                    in_=planes["o", g][32 * q : 32 * q + 4, :].bitcast(I32),
                )

        steps = {"lead": lead, "dv": load_dv, "Lgs": load_gs, "L": load, "pt": pt, "ps": ps, "pi": pi, "pq": pq, "turn": turn, "wq": wq, "mm": mm, "ug": ug, "uh": uh,
                 "dg": dg, "sc": sc, "ua": ua, "us": us, "qi": qi, "qq": qq, "ln": ln, "df": df, "rx": rx, "om": om, "pf": pf, "oc": oc, "oq": oq, "os": store_scales}
        for step in ORDER:
            steps[step[0]](*step[1:])
